import numpy as np, ml_dtypes
CORES = [9,25,41,57]
N = 4
import mx_ref
BF = ml_dtypes.bfloat16
def f(rng, *shape):
    return mx_ref.flush((rng.standard_normal(shape, dtype=np.float32) * np.exp2(rng.integers(-2, 3, shape[:-1] + (1,)))).astype(BF))
def wide(rng, *shape, cols=0):
    v = rng.standard_normal(shape, dtype=np.float32) * np.exp2(rng.integers(-12, 13, shape)).astype(np.float32)
    if cols: v *= np.repeat(np.exp2(rng.integers(-cols, cols + 1, shape[:-2] + (1, shape[-1] // 4))) * (rng.random(shape[:-2] + (1, shape[-1] // 4)) > 0.0625), 4, axis=-1).astype(np.float32)
    return mx_ref.flush(v.astype(BF))
T, CAPP, O = 512, 192, 2
def scores(us, x):
    return mx_ref.matmul(mx_ref.quantize(us), mx_ref.quantize(x))[:8] + np.float32(0.0)
def winners(us, x):
    return np.argmax(np.stack([scores(us[s], x[s]) for s in range(N)]), axis=0)
def fill(rng, n, tot, most):
    n = np.array(n)
    while n.sum() < tot:
        q = rng.integers(0, N)
        if n[q] < most[q]: n[q] += 1
    return rng.permutation(np.repeat(np.arange(N), n))
def deal(rng, full):
    return np.stack([fill(rng, [CAPP if q in full[g] else 0 for q in range(N)], T, [CAPP] * N) for g in range(8)])
def one(rng):
    g, s = rng.integers(0, 8), rng.integers(0, N)
    return deal(rng, [[s] if i == g else [] for i in range(8)])
def heads(rng):
    u, h = np.zeros((8, 16, 128, 4), np.float32), np.arange(8)
    u[h, :, h] = rng.choice([-1.0, 1.0], (8, 16, 4)) * (0.25 + np.abs(rng.standard_normal((8, 16, 4)))) * np.exp2(rng.integers(-2, 3, (8, 16, 1)))
    return np.repeat(u.reshape(1, 128, 512).astype(BF), N, axis=0)
def plant(rng, x, us, wn, big=4, tie=None, zero=None):
    v = np.abs(x.astype(np.float32)).reshape(N, 8, 16, T, 4)
    v[v < 2.0 ** -24] = 0
    h, b = np.arange(8), np.float32(big)
    a = np.sign(us.astype(np.float32)).reshape(8, 16, 128, 4)[h, :, h][:, :, None]
    win = (wn == np.arange(N)[:, None, None])[:, :, None, :, None]
    neg = (rng.random((8, T)) < 0.125)[:, None, :, None]
    c = np.where(rng.random(v.shape, dtype=np.float32) < 0.5, np.float32(-1), np.float32(1))
    t = (np.where(neg, np.where(win, -a, -4 * b * a), np.where(win, b * a, c)) * v).astype(np.float32)
    s = np.stack([scores(us, t[r].reshape(128, 4 * T).astype(BF)) for r in range(N)])
    won = np.take_along_axis(s, wn[None], axis=0)[0]
    lost = np.where(win[:, :, 0, :, 0], -np.inf, s).max(axis=0)
    bad = (~(won - lost > 0.5 * np.abs(won)))[:, None, :, None]
    t = np.where(bad, np.where(win, b * a, -a) * v, t).astype(np.float32)
    if tie is not None:
        best = np.where(win, t, np.float32(0)).sum(axis=0)
        t = np.where(tie[:, None, :, None] & (wn < np.arange(N)[:, None, None])[:, :, None, :, None], best, t)
    if zero is not None: t[:, :, :, zero] = 0
    return t.reshape(N, 128, 4 * T).astype(BF)
def narrow(rng, x, us, wn):
    v, h = x.astype(np.float32).reshape(N, 8, 16, T, 4), np.arange(8)
    u = np.abs(us.astype(np.float32)).reshape(8, 16, 128, 4)[h, :, h]
    i, b = np.unravel_index(u.reshape(8, 64).argmin(axis=1), (16, 4))
    win = wn == np.arange(N)[:, None, None]
    part = np.where(win[:, :, None, :, None], v, np.float32(0)).sum(axis=0)
    p = np.exp2(np.floor(np.log2((u[:, :, None] * np.abs(part)).sum(axis=(1, 3))) - np.log2(u[h, i, b])[:, None]) - 12)
    z = np.stack([np.where(part[g, i[g], :, b[g]] < 0, -p[g], p[g]) for g in range(8)])
    close = np.repeat((rng.permutation(T) < T // 3)[None], 8, axis=0)
    other = (wn + rng.integers(1, N, (8, T))) % N
    hold = ((rng.random((N, 8, T)) < 0.25) | (other == np.arange(N)[:, None, None])) & ~win & close
    held = hold | (win & close)
    t = np.where(held[:, :, None, :, None], part, v).astype(np.float32)
    d = np.where(hold, rng.choice([-0.125, 0.125], (N, 8, T)), 0.0)
    for k in range(2):
        for g in range(8): t[:, g, i[g], :, b[g]] = np.where(held[:, g], z[g] * (1.5 + d[:, g]), t[:, g, i[g], :, b[g]])
        s = np.stack([scores(us, t[r].reshape(128, 4 * T).astype(BF)) for r in range(N)])
        if k == 0: d = np.where(s == np.take_along_axis(s, wn[None], axis=0), 2 * d, d)
    now = np.argmax(s, axis=0)
    for g in range(8):
        for k in range(T):
            n = np.bincount(now[g], minlength=N)
            q = n.argmax()
            if n[q] <= CAPP: break
            j = rng.permutation(np.flatnonzero((now[g] == q) & (wn[g] != q)))[:n[q] - CAPP]
            now[g, j] = wn[g, j]; close[g, j] = False
    return np.where(close[:, None, :, None], t, v).reshape(N, 128, 4 * T).astype(BF)
def draw(rng, wn, **k):
    us = heads(rng)
    return {"x": plant(rng, f(rng, N, 128, 4 * T), us[0], wn, **k), "us": us, "w": f(rng, N, 128, 512 * O)}
def setup_inputs(rng):
    return draw(rng, one(rng))
def setup_inputs_equal(rng):
    e, p = CAPP - 8, rng.permutation(T)
    far = np.stack([fill(rng, [8] + [0] * (N - 1), T - e, [8] + [CAPP] * (N - 1)) for g in range(8)])
    wn = np.concatenate([np.zeros((8, e), int), far], axis=1)[:, p]
    tie = np.repeat(np.concatenate([np.ones(e, bool), np.arange(T - e) % 2 == 0])[None], 8, axis=0)[:, p]
    return draw(rng, wn, tie=tie, zero=(np.arange(T) < 4)[p])
def setup_inputs_full(rng):
    s, k = int(rng.integers(0, N)), T // CAPP
    return draw(rng, deal(rng, [[s] + [q for q in rng.permutation(N).tolist() if q != s][:k - 1] for g in range(8)]))
def setup_inputs_near(rng):
    wn = one(rng)
    d = draw(rng, wn); d["x"] = narrow(rng, d["x"], d["us"][0], wn); return d
def setup_inputs_spread(rng):
    wn, us = one(rng), heads(rng)
    e = np.exp2(rng.integers(-4, 5, (N, 8, 1, T, 1))) * ((rng.random((N, 8, 1, T, 1)) > 0.0625) | (wn == np.arange(N)[:, None, None])[:, :, None, :, None])
    x = wide(rng, N, 128, 4 * T).astype(np.float32).reshape(N, 8, 16, T, 4) * e.astype(np.float32)
    return {"x": plant(rng, x, us[0], wn, big=256), "us": us, "w": f(rng, N, 128, 512 * O)}
def setup_inputs_stretch(rng):
    L = []
    for g in range(8):
        s, a = rng.integers(0, N), rng.choice([0, T - CAPP, rng.integers(0, T - CAPP + 1)])
        far = fill(rng, [0] * N, T - CAPP, [0 if q == s else CAPP for q in range(N)])
        L.append(np.concatenate([far[:a], np.full(CAPP, s), far[a:]]))
    return draw(rng, np.stack(L))
def check_inputs(d):
    b = []
    for k in ("x", "us", "w"):
        v = np.abs(np.asarray(d[k]).astype(np.float32))
        if not ((v == 0) | ((v >= 2.0 ** -30) & (v <= 2.0 ** 30))).all(): b.append(k)
    if b: return b
    u, h = np.array(d["us"]).astype(np.float32), np.arange(8)
    same = (u == u[:1]).all()
    u = u.reshape(N, 8, 16, 128, 4); u[:, h, :, h] = 0
    if not same or (u != 0).any(): b.append("us")
    wn = winners(d["us"], d["x"])
    if max((wn == s).sum(axis=1).max() for s in range(N)) > CAPP: b.append("x")
    return b
def reference(x, us, w):
    wn = winners(us, x)
    M = []
    for s in range(N):
        v = np.where((wn == s)[:, None, :, None], x[s].astype(np.float32).reshape(8, 16, T, 4), np.float32(0))
        M.append(mx_ref.quantize(np.ascontiguousarray(v.reshape(128, 4 * T).astype(BF))))
    y = np.zeros((N, 128, O * T), np.float32)
    for r in range(N):
        for o in range(O):
            W = mx_ref.quantize(np.ascontiguousarray(w[r][:, 512 * o:512 * o + 512]))
            for s in range(N): y[r][:, T * o:T * o + T] += mx_ref.matmul(W, M[s])
    return {"y": y, "wn": np.repeat(wn.astype(np.float32)[None], N, axis=0)}

@@ -1,0 +1,364 @@
+from concourse.mybir import dt, AluOpType, AxisListType, ActivationFunctionType
+
+CAP = 192
+PL = 512
+NR = 4
+RW = NR * CAP
+LW = 1136
+SCRATCH = {
+    "us_sb": ("sbuf", [128, 32], "bfloat16"),
+    "ut": ("sbuf", [128, 4 * 288], "bfloat16"),
+    "uq": ("sbuf", [128, 288], "float8_e4m3fn_x4"),
+    "up": ("sbuf", [128, 288], "uint8"),
+    "xb": ("sbuf", [128, 4 * 608], "bfloat16"),
+    "xq": ("sbuf", [128, 608], "float8_e4m3fn_x4"),
+    "xp": ("sbuf", [128, 608], "uint8"),
+    "zt": ("sbuf", [128, 512], "bfloat16"),
+    "wm": ("sbuf", [128, 8192], "bfloat16"),
+    "wq": ("sbuf", [128, 2048], "float8_e4m3fn_x4"),
+    "wp": ("sbuf", [128, 2048], "uint8"),
+    "cb": ("sbuf", [128, 4 * CAP], "bfloat16"),
+    "lq": ("sbuf", [128, RW], "float8_e4m3fn_x4"),
+    "lp": ("sbuf", [128, RW], "uint8"),
+    "sc": ("sbuf", [128, 128], "float32"),
+    "ip": ("sbuf", [128, 1], "int32"),
+    "i15": ("sbuf", [128, 1], "int32"),
+    "ial": ("sbuf", [128, 1], "int32"),
+    "it3": ("sbuf", [128, 1], "int32"),
+    "alf": ("sbuf", [128, 1], "float32"),
+    "t3f": ("sbuf", [128, 1], "float32"),
+    "a32": ("sbuf", [128, 1], "float32"),
+    "vi": ("sbuf", [128, 512], "float32"),
+    "vv": ("sbuf", [128, 512], "float32"),
+    "bi": ("sbuf", [128, 32], "float32"),
+    "dl": ("sbuf", [128, 32], "float32"),
+    "dc": ("sbuf", [128, 32], "float32"),
+    "ki": ("sbuf", [128, 240], "float32"),
+    "k1": ("sbuf", [128, 240], "float32"),
+    "k2": ("sbuf", [128, 240], "float32"),
+    "kk": ("sbuf", [128, 240], "float32"),
+    "mi": ("sbuf", [128, 128], "float32"),
+    "m16": ("sbuf", [128, 128], "float32"),
+    "ni": ("sbuf", [128, 128], "float32"),
+    "m32": ("sbuf", [128, 128], "float32"),
+    "mx1": ("sbuf", [128, 32], "float32"),
+    "mx2": ("sbuf", [128, 32], "float32"),
+    "cl1": ("sbuf", [128, 32], "float32"),
+    "cl2": ("sbuf", [128, 32], "float32"),
+    "win": ("sbuf", [128, 32], "float32"),
+    "ra": ("sbuf", [128, 32], "float32"),
+    "rt": ("sbuf", [128, 64], "float32"),
+    "ea": ("sbuf", [128, 32], "float32"),
+    "et": ("sbuf", [128, 32], "float32"),
+    "w2": ("sbuf", [128, 32], "float32"),
+    "u2": ("sbuf", [128, 32], "float32"),
+    "ta": ("sbuf", [128, 32], "float32"),
+    "oi": ("sbuf", [128, 32], "int32"),
+    "ou": ("sbuf", [128, 32], "uint16"),
+    "ll": ("sbuf", [128, LW], "float32"),
+    "sl5": ("sbuf", [128, 240], "float32"),
+    "offa": ("sbuf", [128, 48], "uint16"),
+    "m64": ("sbuf", [128, 64], "float32"),
+    "mm": ("sbuf", [128, 32], "float32"),
+    "ne": ("sbuf", [128, 96], "float32"),
+    "q2": ("sbuf", [128, 32], "float32"),
+    "q1": ("sbuf", [128, 32], "float32"),
+    "q0": ("sbuf", [128, 32], "float32"),
+    "wnt": ("sbuf", [128, 32], "float32"),
+    "ww": ("sbuf", [128, 128], "float32"),
+    "rr": ("sbuf", [128, 128], "float32"),
+    "rt4": ("sbuf", [128, 160], "float32"),
+    "e4": ("sbuf", [128, 128], "float32"),
+    "et4": ("sbuf", [128, 128], "float32"),
+    "p4": ("sbuf", [128, 128], "float32"),
+    "pm": ("sbuf", [128, 128], "float32"),
+    "ph": ("sbuf", [128, 64], "float32"),
+    "pi": ("sbuf", [128, 32], "float32"),
+    "ptr": ("sbuf", [128, 32], "float32"),
+    "d2": ("dram", [16, 256], "float32"),
+    "zz": ("sbuf", [128, 256], "float32"),
+    "offb": ("sbuf", [128, 256], "uint16"),
+    "rw": ("sbuf", [128, 16 * RW], "float32"),
+    "g0": ("sbuf", [128, 512], "float32"),
+    "g1": ("sbuf", [128, 512], "float32"),
+    "g7": ("sbuf", [128, 512], "float32"),
+    "ac0": ("sbuf", [128, 512], "float32"),
+    "ac1": ("sbuf", [128, 512], "float32"),
+    "ac2": ("sbuf", [128, 512], "float32"),
+    "ac3": ("sbuf", [128, 512], "float32"),
+}
+for _k in range(8):
+    SCRATCH["ps%d" % _k] = ("psum", [128, 512], "float32")
+SEMAPHORES = (["v", "a", "pv", "pa", "px", "gi", "us", "wn", "d2s", "zs", "ga", "y0", "y1", "y2", "sloc", "cloc"]
+              + ["x%d" % i for i in range(4)] + ["w%d" % i for i in range(4)]
+              + ["s%d" % i for i in range(4)] + ["c%d" % i for i in range(4)])
+
+
+def rank_program(g, core, T, topo):
+    r = T.rank_of(core)
+    if r is None:
+        return
+    A = AluOpType
+    COPY = ActivationFunctionType.Copy
+    IDENT = ActivationFunctionType.Identity
+    Q = {"g": g, "v": g.vector, "a": g.scalar, "p": g.tensor, "s": g.sync}
+    seen = {k: {} for k in Q}
+    cnt = {}
+
+    def need(qn, deps):
+        for s, n in deps:
+            if seen[qn].get(s, 0) < n:
+                Q[qn].wait_ge(T.sem[s], n)
+                seen[qn][s] = n
+
+    def op(qn, deps, call, sem, n=1):
+        need(qn, deps)
+        call().then_inc(T.sem[sem], n)
+        cnt[sem] = cnt.get(sem, 0) + n
+        return (sem, cnt[sem])
+
+    V = g.vector
+    S = g.scalar
+
+    def v(deps, call):
+        return op("v", deps, call, "v")
+
+    def a(deps, call):
+        return op("a", deps, call, "a")
+
+    def dma(qn, deps, out, in_, sem):
+        return op(qn, deps, lambda: Q[qn].dma_start(out, in_), sem, 16)
+
+    peers = [(r + k) % NR for k in (1, 2, 3)]
+    senders = [(r - k) % NR for k in (1, 2, 3)]
+
+    t_us = dma("s", [], T.us_sb[:], T.us[:, 0:32], "us")
+    t_x = {}
+    for i, qn in ((3, "s"), (2, "a"), (1, "s"), (0, "a")):
+        t_x[i] = dma(qn, [], T.xb[:, 512 * i:512 * i + 512], T.x[:, 512 * i:512 * i + 512], "x%d" % i)
+
+    def io(out, pattern, base, cm):
+        return op("g", [], lambda: g.iota(out, pattern, base, cm, allow_small_or_imprecise_dtypes=True), "gi")
+    io(T.ip[:], [[0, 1]], 0, 1)
+    io(T.bi[:], [[1, 32]], 200, 0)
+    io(T.ki[:], [[0, 48], [1, 5]], 0, 0)
+    io(T.mi[:], [[0, 8], [1, 16]], 0, 0)
+    t_small = io(T.ni[:], [[0, 4], [1, 32]], 0, 0)
+    t_vi = io(T.vi[:], [[4, 32], [128, 16]], 0, 0)
+
+    t_zt = v([], lambda: V.memset(T.zt[:], 0.0))
+    v([], lambda: V.memset(T.ut[:], 0.0))
+    v([], lambda: V.memset(T.xb[:, 2048:2432], 0.0))
+    v([], lambda: V.memset(T.ll[:, 0:240], 2048.0))
+    v([], lambda: V.memset(T.rt[:, 0:32], 0.0))
+    t_f = v([], lambda: V.memset(T.rt4[:, 0:32], 0.0))
+    t_z = {}
+    for h in range(4):
+        t_z[h] = v([], lambda: V.memset(T.wm[:, 1024 * h:1024 * h + 1024], 0.0))
+    for h in range(4, 8):
+        for k in range(2):
+            c0 = 1024 * h + 512 * k
+            t_z[h] = a([t_zt], lambda: S.activation(T.wm[:, c0:c0 + 512], T.zt[:], COPY))
+    c1 = v([t_small], lambda: V.tensor_scalar(T.i15[:], T.ip[:], 15, None, A.bitwise_and))
+    c2 = v([], lambda: V.tensor_scalar(T.ial[:], T.ip[:], 15, 2, A.bitwise_and, A.arith_shift_right))
+    c3 = v([], lambda: V.tensor_scalar(T.it3[:], T.ip[:], 3, None, A.bitwise_and))
+    v([], lambda: V.tensor_scalar(T.m16[:], T.mi[:], 0.5, None, A.is_gt))
+    v([], lambda: V.tensor_scalar(T.m32[:], T.ni[:], 0.5, None, A.is_gt))
+    c4 = v([], lambda: V.tensor_scalar(T.k2[:], T.ki[:], 4.0, 4096.0, A.is_equal, A.mult))
+    c5 = v([c1], lambda: V.tensor_scalar(T.a32[:], T.i15[:], 32.0, None, A.mult))
+    c6 = v([c2], lambda: V.tensor_copy(T.alf[:], T.ial[:]))
+    c7 = v([c3], lambda: V.tensor_copy(T.t3f[:], T.it3[:]))
+    v([c5], lambda: V.tensor_scalar(T.dl[:], T.bi[:], T.a32[:], None, A.add))
+    v([], lambda: V.tensor_scalar(T.dc[:], T.bi[:], T.a32[:], -1.3, A.add, A.add))
+    c8 = v([c6], lambda: V.tensor_scalar(T.k1[:], T.ki[:], T.alf[:], 4096.0, A.is_lt, A.mult))
+    t_const = v([c4, c8], lambda: V.tensor_tensor(T.kk[:], T.k1[:], T.k2[:], A.max))
+    t_vv = a([c7, t_vi], lambda: S.activation(T.vv[:], T.vi[:], IDENT, bias=T.t3f[:]))
+
+    t_w = {}
+    for h in range(8):
+        t_w[h // 2] = dma("s", [t_z[h]], T.wm[16 * h:16 * h + 16, 1024 * h:1024 * h + 1024], T.w[16 * h:16 * h + 16, :],
+                          "w%d" % (h // 2))
+
+    for base in (4 * 15, 4 * (144 + 16)):
+        for e in range(4):
+            t_ut = v([t_us, t_f], lambda: V.tensor_copy(T.ut[:, base + e:base + e + 449:64], T.us_sb[:, e:32:4]))
+    t_uq = v([t_ut], lambda: V.quantize_mx(T.uq[:], T.up[:], T.ut[:]))
+    for i in (3, 2, 1, 0):
+        lo, hi = 128 * i, (608 if i == 3 else 128 * i + 128)
+        t_q = v([t_x[i]], lambda: V.quantize_mx(T.xq[:, lo:hi], T.xp[:, lo:hi], T.xb[:, 4 * lo:4 * hi]))
+        need("p", [t_uq, t_q])
+        for k in (4 * i + 3, 4 * i + 2, 4 * i + 1, 4 * i):
+            st = 15 - k if k % 2 else 144 + 16 - k
+            call = lambda: g.tensor.matmul_mx(T.ps0[:, 0:128], T.uq[:, st:st + 128], T.up[:, st:st + 128],
+                                              T.xq[:, 32 * k:32 * k + 128], T.xp[:, 32 * k:32 * k + 128], k == 15, k == 0)
+            if k:
+                call()
+            else:
+                t_sm = op("p", [], call, "px")
+    t_own = v([t_sm], lambda: V.tensor_copy(T.sc[:, 32 * r:32 * r + 32], T.ps0[:, 0:32]))
+
+    def send(dst, out, in_, rsem, lsem):
+        d = T.cores[dst]
+        rid, pid, _se = topo.addr(d)
+        g.remote_dma(out, in_, T.sem[rsem], T.sem[lsem], pid, rid, topo.mask(core, d))
+        cnt[lsem] = cnt.get(lsem, 0) + len(topo.engines(core, d))
+
+    need("g", [t_own])
+    for d in peers:
+        send(d, T.sc[:, 32 * r:32 * r + 32], T.sc[:, 32 * r:32 * r + 32], "s%d" % r, "sloc")
+    n_in = {s: len(topo.engines(T.cores[s], core)) for s in senders}
+
+    for i in range(4):
+        t_wq = v([t_w[i]], lambda: V.quantize_mx(T.wq[:, 512 * i:512 * i + 512], T.wp[:, 512 * i:512 * i + 512],
+                                                 T.wm[:, 2048 * i:2048 * i + 2048]))
+
+    def score(s):
+        return T.sc[:, 32 * s:32 * s + 32]
+
+    def arrived(s):
+        return [("s%d" % s, n_in[s])]
+    conds = []
+    for side, buf, cbuf, cmp in ((lambda s: s < r, T.mx1, T.cl1, A.is_gt), (lambda s: s > r, T.mx2, T.cl2, A.is_ge)):
+        grp = [s for s in senders if side(s)]
+        if not grp:
+            continue
+        cur, tk = score(grp[0]), []
+        need("v", arrived(grp[0]))
+        for n, s in enumerate(grp[1:]):
+            nxt = buf[:] if n == 0 else T.win[:]
+            tk = [v(tk + arrived(s), lambda: V.tensor_tensor(nxt, cur, score(s), A.max))]
+            cur = nxt
+        conds.append((cbuf, v(tk + [t_own], lambda: V.tensor_tensor(cbuf[:], score(r), cur, cmp))))
+    if len(conds) == 2:
+        wn_ = T.win
+        t_win = v([conds[0][1], conds[1][1]], lambda: V.tensor_tensor(T.win[:], T.cl1[:], T.cl2[:], A.mult))
+    else:
+        wn_, t_win = conds[0]
+    m16a, m32a = T.m16[:, 0:32], T.m32[:, 0:32]
+    t1 = v([t_win, t_const], lambda: V.tensor_tensor_scan(T.ra[:], m32a, wn_[:], 0.0, A.mult, A.add))
+    b1 = v([], lambda: V.tensor_tensor(T.w2[:], wn_[:], T.dl[:], A.mult))
+    t2 = v([t1], lambda: V.transpose(T.rt[:, 32:64], T.ra[:]))
+    b2 = v([b1], lambda: V.tensor_tensor(T.u2[:], T.dc[:], T.w2[:], A.subtract))
+    t3 = v([t2], lambda: V.tensor_tensor_scan(T.ea[:], T.rt[:, 31:63], m16a, 0.0, A.add, A.mult))
+    b3 = v([b2], lambda: V.tensor_tensor(T.ta[:], T.u2[:], T.ra[:], A.add))
+    t4 = v([t3], lambda: V.transpose(T.et[:], T.ea[:]))
+    t5 = v([t4, b3], lambda: V.tensor_scalar(T.oi[:], T.ta[:], T.et[:, 31:32], 1.25, A.add, A.mult))
+    t6 = v([t5], lambda: V.tensor_copy(T.ou[:], T.oi[:]))
+    t7 = v([t6, t_vv], lambda: V.tensor_copy(T.ll[:].indirect(T.ou[:]), T.vv[:]))
+    t8 = v([t7], lambda: V.tensor_tensor_scan(T.sl5[:], T.ll[:, 0:240], T.kk[:], 4096.0, A.min, A.max))
+    t9 = v([t8], lambda: V.tensor_copy(T.offa[:], T.sl5[:, 3:240:5]))
+    t10 = a([t9], lambda: S.activation(T.cb[:, 384:768], T.xb[:].indirect(T.offa[:, 24:48]), COPY))
+    t11 = v([t9], lambda: V.tensor_copy(T.cb[:, 0:384], T.xb[:].indirect(T.offa[:, 0:24])))
+    lo = CAP * r
+    t_c = v([t10, t11], lambda: V.quantize_mx(T.lq[:, lo:lo + CAP], T.lp[:, lo:lo + CAP], T.cb[:]))
+    need("g", [t_c])
+    for d in peers:
+        cv, pv_ = T.lq[:, lo:lo + CAP].bitcast(dt.uint8), T.lp[:, lo:lo + CAP]
+        send(d, cv, cv, "c%d" % r, "cloc")
+        send(d, pv_, pv_, "c%d" % r, "cloc")
+
+    for s in senders:
+        need("v", arrived(s))
+    t = v([t_own], lambda: V.tensor_tensor(T.m64[:], T.sc[:, 0:64], T.sc[:, 64:128], A.max))
+    t = v([t], lambda: V.tensor_tensor(T.mm[:], T.m64[:, 0:32], T.m64[:, 32:64], A.max))
+    n2 = v([t], lambda: V.tensor_tensor(T.ne[:, 64:96], score(2), T.mm[:], A.not_equal))
+    n1 = v([], lambda: V.tensor_tensor(T.ne[:, 32:64], score(1), T.mm[:], A.not_equal))
+    t = v([n2], lambda: V.tensor_scalar(T.q2[:], T.ne[:, 64:96], 1.0, None, A.add))
+    n0 = v([], lambda: V.tensor_tensor(T.ne[:, 0:32], score(0), T.mm[:], A.not_equal))
+    t = v([t, n1], lambda: V.tensor_tensor(T.q1[:], T.ne[:, 32:64], T.q2[:], A.mult))
+    t = v([t], lambda: V.tensor_scalar(T.q0[:], T.q1[:], 1.0, None, A.add))
+    t_wn = v([t, n0], lambda: V.tensor_tensor(T.wnt[:], T.ne[:, 0:32], T.q0[:], A.mult))
+    for s in range(NR):
+        t = v([t_wn], lambda: V.tensor_scalar(T.ww[:, 32 * s:32 * s + 32], T.wnt[:], float(s), None, A.is_equal))
+    t = t_rr = v([t], lambda: V.tensor_tensor_scan(T.rr[:], T.m32[:], T.ww[:], 0.0, A.mult, A.add))
+    t = v([t], lambda: V.transpose(T.rt4[:, 32:160], T.rr[:]))
+    t = v([t], lambda: V.tensor_tensor_scan(T.e4[:], T.rt4[:, 31:159], T.m16[:], 0.0, A.add, A.mult))
+    t = v([t], lambda: V.transpose(T.et4[:], T.e4[:]))
+    for s in range(NR):
+        c = 32 * s
+        t4_ = v([t], lambda: V.tensor_scalar(T.p4[:, c:c + 32], T.rr[:, c:c + 32], T.et4[:, c + 31:c + 32],
+                                             float(CAP * s - 1), A.add, A.add))
+    t = v([t4_], lambda: V.tensor_tensor(T.pm[:], T.p4[:], T.ww[:], A.mult))
+    t = v([t], lambda: V.tensor_tensor(T.ph[:], T.pm[:, 0:64], T.pm[:, 64:128], A.add))
+    t = v([t], lambda: V.tensor_tensor(T.pi[:], T.ph[:, 0:32], T.ph[:, 32:64], A.add))
+    t_pt = v([t], lambda: V.transpose(T.ptr[:], T.pi[:]))
+    for ab in range(4):
+        for bh in range(2):
+            p0, c0 = 32 * ab + 16 * bh, 128 * bh + 32 * ab
+            t_d2 = dma("s", [t_pt], T.d2[0:16, c0:c0 + 32], T.ptr[p0:p0 + 16, :], "d2s")
+    for k in range(8):
+        t_zz = dma("s", [t_d2], T.zz[16 * k:16 * k + 16, :], T.d2[:], "zs")
+    dma("s", [t_wn], T.wn[:], T.wnt[:], "wn")
+
+    banks = {"v": [T.ps0, T.ps1, T.ps2, T.ps3], "a": [T.ps4, T.ps5, T.ps6, T.ps7]}
+    hist = {"v": [], "a": []}
+    ready = {}
+
+    def product(s, h, o, e, deps):
+        n = len(hist[e])
+        bank = banks[e][n % 4]
+        old = [hist[e][n - 4]] if n >= 4 else [t_own]
+        w0, c0 = 256 * h + 128 * o, CAP * s
+        tk = op("p", deps + old + [t_wq], lambda: g.tensor.matmul_mx(
+            bank[:, 0:CAP], T.wq[:, w0:w0 + 128], T.wp[:, w0:w0 + 128], T.lq[:, c0:c0 + CAP], T.lp[:, c0:c0 + CAP],
+            True, True), "p" + e)
+        d0 = RW * (2 * h + o) + c0
+        if e == "v":
+            c = v([tk], lambda: V.tensor_copy(T.rw[:, d0:d0 + CAP], bank[:, 0:CAP]))
+        else:
+            c = a([tk], lambda: S.activation(T.rw[:, d0:d0 + CAP], bank[:, 0:CAP], COPY))
+        hist[e].append(c)
+        ready[(s, h, o)] = c
+
+    def window(h, o):
+        d0 = RW * (2 * h + o)
+        return T.rw[:, d0:d0 + RW]
+
+    def rdeps(h, o):
+        return [ready[(s, h, o)] for s in range(NR)]
+
+    jobs = [(h, o) for h in range(8) for o in range(2)]
+    for n, (h, o) in enumerate(jobs):
+        product(r, h, o, "v" if n % 4 == 3 else "a", [t_c])
+    for s in senders[:2]:
+        for n, (h, o) in enumerate(jobs):
+            product(s, h, o, "v" if n % 2 else "a", [("c%d" % s, 2 * n_in[s])])
+    for bh in range(2):
+        t_ob = v([t_zz], lambda: V.tensor_copy(T.offb[:, bh:256:2], T.zz[:, 128 * bh:128 * bh + 128]))
+    s = senders[2]
+    dep = [("c%d" % s, 2 * n_in[s])]
+
+    def gath(out, h, o):
+        return a(rdeps(h, o) + [t_ob], lambda: S.activation(out[:], window(h, o).indirect(T.offb[:, 32 * h:32 * h + 32]), COPY))
+    for h, o, e in ((0, 0, "a"), (1, 0, "v"), (0, 1, "a"), (2, 0, "v")):
+        product(s, h, o, e, dep)
+    t_g0 = gath(T.g0, 0, 0)
+    for h, o, e in ((3, 0, "v"), (4, 0, "a"), (1, 1, "v"), (5, 0, "a"), (2, 1, "v"), (6, 0, "a"), (3, 1, "v"), (7, 0, "a"),
+                    (7, 1, "a")):
+        product(s, h, o, e, dep)
+    t_g1 = gath(T.g1, 0, 1)
+    t_g7 = gath(T.g7, 7, 1)
+    t_ga = op("g", [t_g1, t_g7], lambda: g.dma_start(T.g1[:], T.g7[:], accum_op=A.add), "ga", 16)
+    for h in (4, 5, 6):
+        product(s, h, 1, "a", dep)
+
+    cur, tk = T.g0, [t_g0]
+    for n, h in enumerate(range(1, 8)):
+        out = (T.ac0, T.ac1)[n % 2]
+        tk = [v(tk + rdeps(h, 0) + [t_ob], lambda: V.tensor_tensor(
+            out[:], window(h, 0).indirect(T.offb[:, 32 * h:32 * h + 32]), cur[:], A.add))]
+        cur = out
+    dma("s", tk, T.y[:, 0:512], cur[:], "y0")
+    cur, tk = T.g1, [t_ga]
+    for n, h in enumerate(range(1, 6)):
+        out = (T.ac2, T.ac3)[n % 2]
+        tk = [v(tk + rdeps(h, 1), lambda: V.tensor_tensor(
+            out[:], window(h, 1).indirect(T.offb[:, 32 * h:32 * h + 32]), cur[:], A.add))]
+        cur = out
+    for k in range(2):
+        c0 = 256 * k
+        t_l = v(tk + rdeps(6, 1), lambda: V.tensor_tensor(
+            T.ac3[:, c0:c0 + 256], window(6, 1).indirect(T.offb[:, 192 + 16 * k:192 + 16 * k + 16]), cur[:, c0:c0 + 256], A.add))
+        dma(("s", "a")[k], [t_l], T.y[:, 512 + c0:768 + c0], T.ac3[:, c0:c0 + 256], "y%d" % (1 + k))
+
+    need("g", sorted(cnt.items()))

@@ -1,94 +1,32 @@
-from concourse.mybir import dt, AluOpType, AxisListType, ActivationFunctionType
+from concourse.bass import DstId, RemoteDMATransfer
+from concourse.mybir import dt, AluOpType, ActivationFunctionType
 
 CAP = 192
-PL = 512
 NR = 4
 RW = NR * CAP
 LW = 1136
-SCRATCH = {
-    "us_sb": ("sbuf", [128, 32], "bfloat16"),
-    "ut": ("sbuf", [128, 4 * 288], "bfloat16"),
-    "uq": ("sbuf", [128, 288], "float8_e4m3fn_x4"),
-    "up": ("sbuf", [128, 288], "uint8"),
-    "xb": ("sbuf", [128, 4 * 608], "bfloat16"),
-    "xq": ("sbuf", [128, 608], "float8_e4m3fn_x4"),
-    "xp": ("sbuf", [128, 608], "uint8"),
-    "zt": ("sbuf", [128, 512], "bfloat16"),
-    "wm": ("sbuf", [128, 8192], "bfloat16"),
-    "wq": ("sbuf", [128, 2048], "float8_e4m3fn_x4"),
-    "wp": ("sbuf", [128, 2048], "uint8"),
-    "cb": ("sbuf", [128, 4 * CAP], "bfloat16"),
-    "lq": ("sbuf", [128, RW], "float8_e4m3fn_x4"),
-    "lp": ("sbuf", [128, RW], "uint8"),
-    "sc": ("sbuf", [128, 128], "float32"),
-    "ip": ("sbuf", [128, 1], "int32"),
-    "i15": ("sbuf", [128, 1], "int32"),
-    "ial": ("sbuf", [128, 1], "int32"),
-    "it3": ("sbuf", [128, 1], "int32"),
-    "alf": ("sbuf", [128, 1], "float32"),
-    "t3f": ("sbuf", [128, 1], "float32"),
-    "a32": ("sbuf", [128, 1], "float32"),
-    "vi": ("sbuf", [128, 512], "float32"),
-    "vv": ("sbuf", [128, 512], "float32"),
-    "bi": ("sbuf", [128, 32], "float32"),
-    "dl": ("sbuf", [128, 32], "float32"),
-    "dc": ("sbuf", [128, 32], "float32"),
-    "ki": ("sbuf", [128, 240], "float32"),
-    "k1": ("sbuf", [128, 240], "float32"),
-    "k2": ("sbuf", [128, 240], "float32"),
-    "kk": ("sbuf", [128, 240], "float32"),
-    "mi": ("sbuf", [128, 128], "float32"),
-    "m16": ("sbuf", [128, 128], "float32"),
-    "ni": ("sbuf", [128, 128], "float32"),
-    "m32": ("sbuf", [128, 128], "float32"),
-    "mx1": ("sbuf", [128, 32], "float32"),
-    "mx2": ("sbuf", [128, 32], "float32"),
-    "cl1": ("sbuf", [128, 32], "float32"),
-    "cl2": ("sbuf", [128, 32], "float32"),
-    "win": ("sbuf", [128, 32], "float32"),
-    "ra": ("sbuf", [128, 32], "float32"),
-    "rt": ("sbuf", [128, 64], "float32"),
-    "ea": ("sbuf", [128, 32], "float32"),
-    "et": ("sbuf", [128, 32], "float32"),
-    "w2": ("sbuf", [128, 32], "float32"),
-    "u2": ("sbuf", [128, 32], "float32"),
-    "ta": ("sbuf", [128, 32], "float32"),
-    "oi": ("sbuf", [128, 32], "int32"),
-    "ou": ("sbuf", [128, 32], "uint16"),
-    "ll": ("sbuf", [128, LW], "float32"),
-    "sl5": ("sbuf", [128, 240], "float32"),
-    "offa": ("sbuf", [128, 48], "uint16"),
-    "m64": ("sbuf", [128, 64], "float32"),
-    "mm": ("sbuf", [128, 32], "float32"),
-    "ne": ("sbuf", [128, 96], "float32"),
-    "q2": ("sbuf", [128, 32], "float32"),
-    "q1": ("sbuf", [128, 32], "float32"),
-    "q0": ("sbuf", [128, 32], "float32"),
-    "wnt": ("sbuf", [128, 32], "float32"),
-    "ww": ("sbuf", [128, 128], "float32"),
-    "rr": ("sbuf", [128, 128], "float32"),
-    "rt4": ("sbuf", [128, 160], "float32"),
-    "e4": ("sbuf", [128, 128], "float32"),
-    "et4": ("sbuf", [128, 128], "float32"),
-    "p4": ("sbuf", [128, 128], "float32"),
-    "pm": ("sbuf", [128, 128], "float32"),
-    "ph": ("sbuf", [128, 64], "float32"),
-    "pi": ("sbuf", [128, 32], "float32"),
-    "ptr": ("sbuf", [128, 32], "float32"),
-    "d2": ("dram", [16, 256], "float32"),
-    "zz": ("sbuf", [128, 256], "float32"),
-    "offb": ("sbuf", [128, 256], "uint16"),
-    "rw": ("sbuf", [128, 16 * RW], "float32"),
-    "g0": ("sbuf", [128, 512], "float32"),
-    "g1": ("sbuf", [128, 512], "float32"),
-    "g7": ("sbuf", [128, 512], "float32"),
-    "ac0": ("sbuf", [128, 512], "float32"),
-    "ac1": ("sbuf", [128, 512], "float32"),
-    "ac2": ("sbuf", [128, 512], "float32"),
-    "ac3": ("sbuf", [128, 512], "float32"),
+F, I32, U16, BF, X4, U8 = "float32", "int32", "uint16", "bfloat16", "float8_e4m3fn_x4", "uint8"
+_sb = {
+    "us_sb": (32, BF), "ut": (4 * 288, BF), "uq": (288, X4), "up": (288, U8),
+    "xb": (4 * 608, BF), "xq": (608, X4), "xp": (608, U8),
+    "zt": (512, BF), "wm": (8192, BF), "wq": (2048, X4), "wp": (2048, U8),
+    "cb": (4 * CAP, BF), "lq": (RW, X4), "lp": (RW, U8), "sc": (128, F),
+    "ip": (1, I32), "i15": (1, I32), "ial": (1, I32), "it3": (1, I32), "alf": (1, F), "t3f": (1, F), "a32": (1, F),
+    "vi": (512, F), "vv": (512, F), "bi": (32, F), "dl": (32, F), "dc": (32, F), "ki": (240, F), "k1": (240, F), "k2": (240, F),
+    "kk": (240, F), "mi": (128, F), "m16": (128, F), "ni": (128, F), "m32": (128, F),
+    "mx1": (32, F), "mx2": (32, F), "cl1": (32, F), "cl2": (32, F), "win": (32, F), "ra": (32, F), "rt": (64, F), "ea": (32, F),
+    "et": (32, F), "w2": (32, F), "u2": (32, F), "ta": (32, F), "oi": (32, I32), "ou": (32, U16), "ll": (LW, F), "sl5": (240, F),
+    "offa": (48, U16),
+    "m64": (64, F), "mm": (32, F), "ne": (96, F), "q2": (32, F), "q1": (32, F), "q0": (32, F), "wnt": (32, F), "ww": (128, F),
+    "rr": (128, F), "rt4": (160, F), "e4": (128, F), "et4": (128, F), "p4": (128, F), "pm": (128, F), "ph": (64, F), "pi": (32, F),
+    "ptr": (32, F), "zz": (256, F), "offb": (256, U16),
+    "rw": (16 * RW, F), "g0": (512, F), "g1": (512, F), "g5": (512, F), "g6": (512, F), "ac0": (512, F), "ac1": (512, F),
+    "ac2": (512, F), "ac3": (512, F),
 }
+SCRATCH = {k: ("sbuf", [128, n], d) for k, (n, d) in _sb.items()}
+SCRATCH["d2"] = ("dram", [16, 256], F)
 for _k in range(8):
-    SCRATCH["ps%d" % _k] = ("psum", [128, 512], "float32")
+    SCRATCH["ps%d" % _k] = ("psum", [128, 512], F)
 SEMAPHORES = (["v", "a", "pv", "pa", "px", "gi", "us", "wn", "d2s", "zs", "ga", "y0", "y1", "y2", "sloc", "cloc"]
               + ["x%d" % i for i in range(4)] + ["w%d" % i for i in range(4)]
               + ["s%d" % i for i in range(4)] + ["c%d" % i for i in range(4)])
@@ -153,26 +91,12 @@ def rank_program(g, core, T, topo):
     v([], lambda: V.memset(T.rt[:, 0:32], 0.0))
     t_f = v([], lambda: V.memset(T.rt4[:, 0:32], 0.0))
     t_z = {}
-    for h in range(4):
+    for h in range(3):
         t_z[h] = v([], lambda: V.memset(T.wm[:, 1024 * h:1024 * h + 1024], 0.0))
-    for h in range(4, 8):
+    for h in range(3, 8):
         for k in range(2):
             c0 = 1024 * h + 512 * k
             t_z[h] = a([t_zt], lambda: S.activation(T.wm[:, c0:c0 + 512], T.zt[:], COPY))
-    c1 = v([t_small], lambda: V.tensor_scalar(T.i15[:], T.ip[:], 15, None, A.bitwise_and))
-    c2 = v([], lambda: V.tensor_scalar(T.ial[:], T.ip[:], 15, 2, A.bitwise_and, A.arith_shift_right))
-    c3 = v([], lambda: V.tensor_scalar(T.it3[:], T.ip[:], 3, None, A.bitwise_and))
-    v([], lambda: V.tensor_scalar(T.m16[:], T.mi[:], 0.5, None, A.is_gt))
-    v([], lambda: V.tensor_scalar(T.m32[:], T.ni[:], 0.5, None, A.is_gt))
-    c4 = v([], lambda: V.tensor_scalar(T.k2[:], T.ki[:], 4.0, 4096.0, A.is_equal, A.mult))
-    c5 = v([c1], lambda: V.tensor_scalar(T.a32[:], T.i15[:], 32.0, None, A.mult))
-    c6 = v([c2], lambda: V.tensor_copy(T.alf[:], T.ial[:]))
-    c7 = v([c3], lambda: V.tensor_copy(T.t3f[:], T.it3[:]))
-    v([c5], lambda: V.tensor_scalar(T.dl[:], T.bi[:], T.a32[:], None, A.add))
-    v([], lambda: V.tensor_scalar(T.dc[:], T.bi[:], T.a32[:], -1.3, A.add, A.add))
-    c8 = v([c6], lambda: V.tensor_scalar(T.k1[:], T.ki[:], T.alf[:], 4096.0, A.is_lt, A.mult))
-    t_const = v([c4, c8], lambda: V.tensor_tensor(T.kk[:], T.k1[:], T.k2[:], A.max))
-    t_vv = a([c7, t_vi], lambda: S.activation(T.vv[:], T.vi[:], IDENT, bias=T.t3f[:]))
 
     t_w = {}
     for h in range(8):
@@ -197,20 +121,43 @@ def rank_program(g, core, T, topo):
                 t_sm = op("p", [], call, "px")
     t_own = v([t_sm], lambda: V.tensor_copy(T.sc[:, 32 * r:32 * r + 32], T.ps0[:, 0:32]))
 
-    def send(dst, out, in_, rsem, lsem):
+    def send(dst, view, rsem, lsem):
         d = T.cores[dst]
         rid, pid, _se = topo.addr(d)
-        g.remote_dma(out, in_, T.sem[rsem], T.sem[lsem], pid, rid, topo.mask(core, d))
+        g.remote_dma(view, view, T.sem[rsem], T.sem[lsem], pid, rid, topo.mask(core, d))
         cnt[lsem] = cnt.get(lsem, 0) + len(topo.engines(core, d))
 
+    def send_all(view, rsem, lsem):
+        ds = [T.cores[d] for d in peers]
+        ids = [DstId(rid=topo.addr(d)[0], pnc=topo.addr(d)[1]) for d in ds]
+        g.remote_dma_fused([RemoteDMATransfer(dst_ids=ids, dma_engine_mask=topo.mask(core, ds[0]), remote_sem=T.sem[rsem],
+                                              srcs=[view], dsts=[view] * 3)], local_sem=T.sem[lsem])
+        cnt[lsem] = cnt.get(lsem, 0) + len(topo.engines(core, ds[0]))
+
     need("g", [t_own])
-    for d in peers:
-        send(d, T.sc[:, 32 * r:32 * r + 32], T.sc[:, 32 * r:32 * r + 32], "s%d" % r, "sloc")
+    send_all(T.sc[:, 32 * r:32 * r + 32], "s%d" % r, "sloc")
     n_in = {s: len(topo.engines(T.cores[s], core)) for s in senders}
 
-    for i in range(4):
-        t_wq = v([t_w[i]], lambda: V.quantize_mx(T.wq[:, 512 * i:512 * i + 512], T.wp[:, 512 * i:512 * i + 512],
+    c1 = v([t_small], lambda: V.tensor_scalar(T.i15[:], T.ip[:], 15, None, A.bitwise_and))
+    c2 = v([], lambda: V.tensor_scalar(T.ial[:], T.ip[:], 15, 2, A.bitwise_and, A.arith_shift_right))
+    c3 = v([], lambda: V.tensor_scalar(T.it3[:], T.ip[:], 3, None, A.bitwise_and))
+    v([], lambda: V.tensor_scalar(T.m16[:], T.mi[:], 0.5, None, A.is_gt))
+    v([], lambda: V.tensor_scalar(T.m32[:], T.ni[:], 0.5, None, A.is_gt))
+    c4 = v([], lambda: V.tensor_scalar(T.k2[:], T.ki[:], 4.0, 4096.0, A.is_equal, A.mult))
+    c5 = v([c1], lambda: V.tensor_scalar(T.a32[:], T.i15[:], 32.0, None, A.mult))
+    c6 = v([c2], lambda: V.tensor_copy(T.alf[:], T.ial[:]))
+    c7 = v([c3], lambda: V.tensor_copy(T.t3f[:], T.it3[:]))
+    v([c5], lambda: V.tensor_scalar(T.dl[:], T.bi[:], T.a32[:], None, A.add))
+    v([], lambda: V.tensor_scalar(T.dc[:], T.bi[:], T.a32[:], -1.3, A.add, A.add))
+    c8 = v([c6], lambda: V.tensor_scalar(T.k1[:], T.ki[:], T.alf[:], 4096.0, A.is_lt, A.mult))
+    t_const = v([c4, c8], lambda: V.tensor_tensor(T.kk[:], T.k1[:], T.k2[:], A.max))
+    t_vv = a([c7, t_vi], lambda: S.activation(T.vv[:], T.vi[:], IDENT, bias=T.t3f[:]))
+
+    def quant_w(i):
+        return v([t_w[i]], lambda: V.quantize_mx(T.wq[:, 512 * i:512 * i + 512], T.wp[:, 512 * i:512 * i + 512],
                                                  T.wm[:, 2048 * i:2048 * i + 2048]))
+    for i in range(3):
+        t_wq = quant_w(i)
 
     def score(s):
         return T.sc[:, 32 * s:32 * s + 32]
@@ -242,43 +189,41 @@ def rank_program(g, core, T, topo):
     t3 = v([t2], lambda: V.tensor_tensor_scan(T.ea[:], T.rt[:, 31:63], m16a, 0.0, A.add, A.mult))
     b3 = v([b2], lambda: V.tensor_tensor(T.ta[:], T.u2[:], T.ra[:], A.add))
     t4 = v([t3], lambda: V.transpose(T.et[:], T.ea[:]))
+    m1 = v([], lambda: V.tensor_tensor(T.m64[:], T.sc[:, 0:64], T.sc[:, 64:128], A.max))
     t5 = v([t4, b3], lambda: V.tensor_scalar(T.oi[:], T.ta[:], T.et[:, 31:32], 1.25, A.add, A.mult))
+    m2 = v([m1], lambda: V.tensor_tensor(T.mm[:], T.m64[:, 0:32], T.m64[:, 32:64], A.max))
     t6 = v([t5], lambda: V.tensor_copy(T.ou[:], T.oi[:]))
+    n2 = v([m2], lambda: V.tensor_tensor(T.ne[:, 64:96], score(2), T.mm[:], A.not_equal))
     t7 = v([t6, t_vv], lambda: V.tensor_copy(T.ll[:].indirect(T.ou[:]), T.vv[:]))
+    n1 = v([], lambda: V.tensor_tensor(T.ne[:, 32:64], score(1), T.mm[:], A.not_equal))
     t8 = v([t7], lambda: V.tensor_tensor_scan(T.sl5[:], T.ll[:, 0:240], T.kk[:], 4096.0, A.min, A.max))
+    n0 = v([], lambda: V.tensor_tensor(T.ne[:, 0:32], score(0), T.mm[:], A.not_equal))
     t9 = v([t8], lambda: V.tensor_copy(T.offa[:], T.sl5[:, 3:240:5]))
+    q2 = v([n2], lambda: V.tensor_scalar(T.q2[:], T.ne[:, 64:96], 1.0, None, A.add))
     t10 = a([t9], lambda: S.activation(T.cb[:, 384:768], T.xb[:].indirect(T.offa[:, 24:48]), COPY))
     t11 = v([t9], lambda: V.tensor_copy(T.cb[:, 0:384], T.xb[:].indirect(T.offa[:, 0:24])))
+    q1 = v([q2, n1], lambda: V.tensor_tensor(T.q1[:], T.ne[:, 32:64], T.q2[:], A.mult))
     lo = CAP * r
     t_c = v([t10, t11], lambda: V.quantize_mx(T.lq[:, lo:lo + CAP], T.lp[:, lo:lo + CAP], T.cb[:]))
     need("g", [t_c])
     for d in peers:
-        cv, pv_ = T.lq[:, lo:lo + CAP].bitcast(dt.uint8), T.lp[:, lo:lo + CAP]
-        send(d, cv, cv, "c%d" % r, "cloc")
-        send(d, pv_, pv_, "c%d" % r, "cloc")
+        send(d, T.lq[:, lo:lo + CAP].bitcast(dt.uint8), "c%d" % r, "cloc")
+        send(d, T.lp[:, lo:lo + CAP], "c%d" % r, "cloc")
+    t_wq3 = quant_w(3)
 
-    for s in senders:
-        need("v", arrived(s))
-    t = v([t_own], lambda: V.tensor_tensor(T.m64[:], T.sc[:, 0:64], T.sc[:, 64:128], A.max))
-    t = v([t], lambda: V.tensor_tensor(T.mm[:], T.m64[:, 0:32], T.m64[:, 32:64], A.max))
-    n2 = v([t], lambda: V.tensor_tensor(T.ne[:, 64:96], score(2), T.mm[:], A.not_equal))
-    n1 = v([], lambda: V.tensor_tensor(T.ne[:, 32:64], score(1), T.mm[:], A.not_equal))
-    t = v([n2], lambda: V.tensor_scalar(T.q2[:], T.ne[:, 64:96], 1.0, None, A.add))
-    n0 = v([], lambda: V.tensor_tensor(T.ne[:, 0:32], score(0), T.mm[:], A.not_equal))
-    t = v([t, n1], lambda: V.tensor_tensor(T.q1[:], T.ne[:, 32:64], T.q2[:], A.mult))
-    t = v([t], lambda: V.tensor_scalar(T.q0[:], T.q1[:], 1.0, None, A.add))
+    t = v([q1], lambda: V.tensor_scalar(T.q0[:], T.q1[:], 1.0, None, A.add))
     t_wn = v([t, n0], lambda: V.tensor_tensor(T.wnt[:], T.ne[:, 0:32], T.q0[:], A.mult))
     for s in range(NR):
         t = v([t_wn], lambda: V.tensor_scalar(T.ww[:, 32 * s:32 * s + 32], T.wnt[:], float(s), None, A.is_equal))
-    t = t_rr = v([t], lambda: V.tensor_tensor_scan(T.rr[:], T.m32[:], T.ww[:], 0.0, A.mult, A.add))
+    t = v([t], lambda: V.tensor_tensor_scan(T.rr[:], T.m32[:], T.ww[:], 0.0, A.mult, A.add))
     t = v([t], lambda: V.transpose(T.rt4[:, 32:160], T.rr[:]))
     t = v([t], lambda: V.tensor_tensor_scan(T.e4[:], T.rt4[:, 31:159], T.m16[:], 0.0, A.add, A.mult))
     t = v([t], lambda: V.transpose(T.et4[:], T.e4[:]))
     for s in range(NR):
         c = 32 * s
-        t4_ = v([t], lambda: V.tensor_scalar(T.p4[:, c:c + 32], T.rr[:, c:c + 32], T.et4[:, c + 31:c + 32],
-                                             float(CAP * s - 1), A.add, A.add))
-    t = v([t4_], lambda: V.tensor_tensor(T.pm[:], T.p4[:], T.ww[:], A.mult))
+        tp = v([t], lambda: V.tensor_scalar(T.p4[:, c:c + 32], T.rr[:, c:c + 32], T.et4[:, c + 31:c + 32],
+                                            float(CAP * s - 1), A.add, A.add))
+    t = v([tp], lambda: V.tensor_tensor(T.pm[:], T.p4[:], T.ww[:], A.mult))
     t = v([t], lambda: V.tensor_tensor(T.ph[:], T.pm[:, 0:64], T.pm[:, 64:128], A.add))
     t = v([t], lambda: V.tensor_tensor(T.pi[:], T.ph[:, 0:32], T.ph[:, 32:64], A.add))
     t_pt = v([t], lambda: V.transpose(T.ptr[:], T.pi[:]))
@@ -299,7 +244,7 @@ def rank_program(g, core, T, topo):
         bank = banks[e][n % 4]
         old = [hist[e][n - 4]] if n >= 4 else [t_own]
         w0, c0 = 256 * h + 128 * o, CAP * s
-        tk = op("p", deps + old + [t_wq], lambda: g.tensor.matmul_mx(
+        tk = op("p", deps + old + [t_wq if h < 6 else t_wq3], lambda: g.tensor.matmul_mx(
             bank[:, 0:CAP], T.wq[:, w0:w0 + 128], T.wp[:, w0:w0 + 128], T.lq[:, c0:c0 + CAP], T.lp[:, c0:c0 + CAP],
             True, True), "p" + e)
         d0 = RW * (2 * h + o) + c0
@@ -330,35 +275,37 @@ def rank_program(g, core, T, topo):
 
     def gath(out, h, o):
         return a(rdeps(h, o) + [t_ob], lambda: S.activation(out[:], window(h, o).indirect(T.offb[:, 32 * h:32 * h + 32]), COPY))
-    for h, o, e in ((0, 0, "a"), (1, 0, "v"), (0, 1, "a"), (2, 0, "v")):
+    for h, o, e in ((7, 0, "a"), (0, 0, "v"), (1, 0, "v")):
         product(s, h, o, e, dep)
-    t_g0 = gath(T.g0, 0, 0)
-    for h, o, e in ((3, 0, "v"), (4, 0, "a"), (1, 1, "v"), (5, 0, "a"), (2, 1, "v"), (6, 0, "a"), (3, 1, "v"), (7, 0, "a"),
-                    (7, 1, "a")):
+    t_g0 = gath(T.g0, 7, 0)
+    for h, o, e in ((5, 0, "a"), (2, 0, "v"), (3, 0, "v"), (6, 0, "a"), (4, 0, "v"), (0, 1, "v"), (1, 1, "v")):
         product(s, h, o, e, dep)
-    t_g1 = gath(T.g1, 0, 1)
-    t_g7 = gath(T.g7, 7, 1)
-    t_ga = op("g", [t_g1, t_g7], lambda: g.dma_start(T.g1[:], T.g7[:], accum_op=A.add), "ga", 16)
-    for h in (4, 5, 6):
+    t_g5 = gath(T.g5, 5, 0)
+    t_g6 = gath(T.g6, 6, 0)
+    t_ga = op("g", [t_g5, t_g6], lambda: g.dma_start(T.g6[:], T.g5[:], accum_op=A.add), "ga", 16)
+    product(s, 7, 1, "a", dep)
+    t_g1 = gath(T.g1, 7, 1)
+    for h in (2, 3, 4, 5, 6):
         product(s, h, 1, "a", dep)
 
     cur, tk = T.g0, [t_g0]
-    for n, h in enumerate(range(1, 8)):
-        out = (T.ac0, T.ac1)[n % 2]
+    for h in range(5):
+        out = (T.ac0, T.ac1)[h % 2]
         tk = [v(tk + rdeps(h, 0) + [t_ob], lambda: V.tensor_tensor(
             out[:], window(h, 0).indirect(T.offb[:, 32 * h:32 * h + 32]), cur[:], A.add))]
         cur = out
-    dma("s", tk, T.y[:, 0:512], cur[:], "y0")
-    cur, tk = T.g1, [t_ga]
-    for n, h in enumerate(range(1, 6)):
-        out = (T.ac2, T.ac3)[n % 2]
+    t_y0 = dma("s", tk, T.y[:, 0:512], cur[:], "y0")
+    op("g", [t_ga, t_y0], lambda: g.dma_start(T.y[:, 0:512], T.g6[:], accum_op=A.add), "ga", 16)
+    cur, tk = T.g1, [t_g1]
+    for h in range(6):
+        out = (T.ac2, T.ac3)[h % 2]
         tk = [v(tk + rdeps(h, 1), lambda: V.tensor_tensor(
             out[:], window(h, 1).indirect(T.offb[:, 32 * h:32 * h + 32]), cur[:], A.add))]
         cur = out
     for k in range(2):
         c0 = 256 * k
         t_l = v(tk + rdeps(6, 1), lambda: V.tensor_tensor(
-            T.ac3[:, c0:c0 + 256], window(6, 1).indirect(T.offb[:, 192 + 16 * k:192 + 16 * k + 16]), cur[:, c0:c0 + 256], A.add))
-        dma(("s", "a")[k], [t_l], T.y[:, 512 + c0:768 + c0], T.ac3[:, c0:c0 + 256], "y%d" % (1 + k))
+            T.ac2[:, c0:c0 + 256], window(6, 1).indirect(T.offb[:, 192 + 16 * k:192 + 16 * k + 16]), cur[:, c0:c0 + 256], A.add))
+        dma(("s", "a")[k], [t_l], T.y[:, 512 + c0:768 + c0], T.ac2[:, c0:c0 + 256], "y%d" % (1 + k))
 
     need("g", sorted(cnt.items()))

from concourse.bass import DstId, RemoteDMATransfer
from concourse.mybir import dt, AluOpType, ActivationFunctionType

CAP = 192
NR = 4
RW = NR * CAP
LW = 1136
F, I32, U16, BF, X4, U8 = "float32", "int32", "uint16", "bfloat16", "float8_e4m3fn_x4", "uint8"
_sb = {
    "us_sb": (32, BF), "ut": (4 * 288, BF), "uq": (288, X4), "up": (288, U8),
    "xb": (4 * 608, BF), "xq": (608, X4), "xp": (608, U8),
    "zt": (512, BF), "wm": (8192, BF), "wq": (2048, X4), "wp": (2048, U8),
    "cb": (4 * CAP, BF), "lq": (RW, X4), "lp": (RW, U8), "sc": (128, F),
    "ip": (1, I32), "i15": (1, I32), "ial": (1, I32), "it3": (1, I32), "alf": (1, F), "t3f": (1, F), "a32": (1, F),
    "vi": (512, F), "vv": (512, F), "bi": (32, F), "dl": (32, F), "dc": (32, F), "ki": (240, F), "k1": (240, F), "k2": (240, F),
    "kk": (240, F), "mi": (128, F), "m16": (128, F), "ni": (128, F), "m32": (128, F),
    "mx1": (32, F), "mx2": (32, F), "cl1": (32, F), "cl2": (32, F), "win": (32, F), "ra": (32, F), "rt": (64, F), "ea": (32, F),
    "et": (32, F), "w2": (32, F), "u2": (32, F), "ta": (32, F), "oi": (32, I32), "ou": (32, U16), "ll": (LW, F), "sl5": (240, F),
    "offa": (48, U16),
    "m64": (64, F), "mm": (32, F), "ne": (96, F), "q2": (32, F), "q1": (32, F), "q0": (32, F), "wnt": (32, F), "ww": (128, F),
    "rr": (128, F), "rt4": (160, F), "e4": (128, F), "et4": (128, F), "p4": (128, F), "pm": (128, F), "ph": (64, F), "pi": (32, F),
    "ptr": (32, F), "zz": (256, F), "offb": (256, U16),
    "rw": (16 * RW, F), "g0": (512, F), "g1": (512, F), "g5": (512, F), "g6": (512, F), "ac0": (512, F), "ac1": (512, F),
    "ac2": (512, F), "ac3": (512, F),
}
SCRATCH = {k: ("sbuf", [128, n], d) for k, (n, d) in _sb.items()}
SCRATCH["d2"] = ("dram", [16, 256], F)
for _k in range(8):
    SCRATCH["ps%d" % _k] = ("psum", [128, 512], F)
SEMAPHORES = (["v", "a", "pv", "pa", "px", "gi", "us", "wn", "d2s", "zs", "ga", "y0", "y1", "y2", "sloc", "cloc"]
              + ["x%d" % i for i in range(4)] + ["w%d" % i for i in range(4)]
              + ["s%d" % i for i in range(4)] + ["c%d" % i for i in range(4)])


def rank_program(g, core, T, topo):
    r = T.rank_of(core)
    if r is None:
        return
    A = AluOpType
    COPY = ActivationFunctionType.Copy
    IDENT = ActivationFunctionType.Identity
    Q = {"g": g, "v": g.vector, "a": g.scalar, "p": g.tensor, "s": g.sync}
    seen = {k: {} for k in Q}
    cnt = {}

    def need(qn, deps):
        for s, n in deps:
            if seen[qn].get(s, 0) < n:
                Q[qn].wait_ge(T.sem[s], n)
                seen[qn][s] = n

    def op(qn, deps, call, sem, n=1):
        need(qn, deps)
        call().then_inc(T.sem[sem], n)
        cnt[sem] = cnt.get(sem, 0) + n
        return (sem, cnt[sem])

    V = g.vector
    S = g.scalar

    def v(deps, call):
        return op("v", deps, call, "v")

    def a(deps, call):
        return op("a", deps, call, "a")

    def dma(qn, deps, out, in_, sem):
        return op(qn, deps, lambda: Q[qn].dma_start(out, in_), sem, 16)

    peers = [(r + k) % NR for k in (1, 2, 3)]
    senders = [(r - k) % NR for k in (1, 2, 3)]

    t_us = dma("s", [], T.us_sb[:], T.us[:, 0:32], "us")
    t_x = {}
    for i, qn in ((3, "s"), (2, "a"), (1, "s"), (0, "a")):
        t_x[i] = dma(qn, [], T.xb[:, 512 * i:512 * i + 512], T.x[:, 512 * i:512 * i + 512], "x%d" % i)

    def io(out, pattern, base, cm):
        return op("g", [], lambda: g.iota(out, pattern, base, cm, allow_small_or_imprecise_dtypes=True), "gi")
    io(T.ip[:], [[0, 1]], 0, 1)
    io(T.bi[:], [[1, 32]], 200, 0)
    io(T.ki[:], [[0, 48], [1, 5]], 0, 0)
    io(T.mi[:], [[0, 8], [1, 16]], 0, 0)
    t_small = io(T.ni[:], [[0, 4], [1, 32]], 0, 0)
    t_vi = io(T.vi[:], [[4, 32], [128, 16]], 0, 0)

    t_zt = v([], lambda: V.memset(T.zt[:], 0.0))
    v([], lambda: V.memset(T.ut[:], 0.0))
    v([], lambda: V.memset(T.xb[:, 2048:2432], 0.0))
    v([], lambda: V.memset(T.ll[:, 0:240], 2048.0))
    v([], lambda: V.memset(T.rt[:, 0:32], 0.0))
    t_f = v([], lambda: V.memset(T.rt4[:, 0:32], 0.0))
    t_z = {}
    for h in range(3):
        t_z[h] = v([], lambda: V.memset(T.wm[:, 1024 * h:1024 * h + 1024], 0.0))
    for h in range(3, 8):
        for k in range(2):
            c0 = 1024 * h + 512 * k
            t_z[h] = a([t_zt], lambda: S.activation(T.wm[:, c0:c0 + 512], T.zt[:], COPY))

    t_w = {}
    for h in range(8):
        t_w[h // 2] = dma("s", [t_z[h]], T.wm[16 * h:16 * h + 16, 1024 * h:1024 * h + 1024], T.w[16 * h:16 * h + 16, :],
                          "w%d" % (h // 2))

    for base in (4 * 15, 4 * (144 + 16)):
        for e in range(4):
            t_ut = v([t_us, t_f], lambda: V.tensor_copy(T.ut[:, base + e:base + e + 449:64], T.us_sb[:, e:32:4]))
    t_uq = v([t_ut], lambda: V.quantize_mx(T.uq[:], T.up[:], T.ut[:]))
    for i in (3, 2, 1, 0):
        lo, hi = 128 * i, (608 if i == 3 else 128 * i + 128)
        t_q = v([t_x[i]], lambda: V.quantize_mx(T.xq[:, lo:hi], T.xp[:, lo:hi], T.xb[:, 4 * lo:4 * hi]))
        need("p", [t_uq, t_q])
        for k in (4 * i + 3, 4 * i + 2, 4 * i + 1, 4 * i):
            st = 15 - k if k % 2 else 144 + 16 - k
            call = lambda: g.tensor.matmul_mx(T.ps0[:, 0:128], T.uq[:, st:st + 128], T.up[:, st:st + 128],
                                              T.xq[:, 32 * k:32 * k + 128], T.xp[:, 32 * k:32 * k + 128], k == 15, k == 0)
            if k:
                call()
            else:
                t_sm = op("p", [], call, "px")
    t_own = v([t_sm], lambda: V.tensor_copy(T.sc[:, 32 * r:32 * r + 32], T.ps0[:, 0:32]))

    def send(dst, view, rsem, lsem):
        d = T.cores[dst]
        rid, pid, _se = topo.addr(d)
        g.remote_dma(view, view, T.sem[rsem], T.sem[lsem], pid, rid, topo.mask(core, d))
        cnt[lsem] = cnt.get(lsem, 0) + len(topo.engines(core, d))

    def send_all(view, rsem, lsem):
        ds = [T.cores[d] for d in peers]
        ids = [DstId(rid=topo.addr(d)[0], pnc=topo.addr(d)[1]) for d in ds]
        g.remote_dma_fused([RemoteDMATransfer(dst_ids=ids, dma_engine_mask=topo.mask(core, ds[0]), remote_sem=T.sem[rsem],
                                              srcs=[view], dsts=[view] * 3)], local_sem=T.sem[lsem])
        cnt[lsem] = cnt.get(lsem, 0) + len(topo.engines(core, ds[0]))

    need("g", [t_own])
    send_all(T.sc[:, 32 * r:32 * r + 32], "s%d" % r, "sloc")
    n_in = {s: len(topo.engines(T.cores[s], core)) for s in senders}

    c1 = v([t_small], lambda: V.tensor_scalar(T.i15[:], T.ip[:], 15, None, A.bitwise_and))
    c2 = v([], lambda: V.tensor_scalar(T.ial[:], T.ip[:], 15, 2, A.bitwise_and, A.arith_shift_right))
    c3 = v([], lambda: V.tensor_scalar(T.it3[:], T.ip[:], 3, None, A.bitwise_and))
    v([], lambda: V.tensor_scalar(T.m16[:], T.mi[:], 0.5, None, A.is_gt))
    v([], lambda: V.tensor_scalar(T.m32[:], T.ni[:], 0.5, None, A.is_gt))
    c4 = v([], lambda: V.tensor_scalar(T.k2[:], T.ki[:], 4.0, 4096.0, A.is_equal, A.mult))
    c5 = v([c1], lambda: V.tensor_scalar(T.a32[:], T.i15[:], 32.0, None, A.mult))
    c6 = v([c2], lambda: V.tensor_copy(T.alf[:], T.ial[:]))
    c7 = v([c3], lambda: V.tensor_copy(T.t3f[:], T.it3[:]))
    v([c5], lambda: V.tensor_scalar(T.dl[:], T.bi[:], T.a32[:], None, A.add))
    v([], lambda: V.tensor_scalar(T.dc[:], T.bi[:], T.a32[:], -1.3, A.add, A.add))
    c8 = v([c6], lambda: V.tensor_scalar(T.k1[:], T.ki[:], T.alf[:], 4096.0, A.is_lt, A.mult))
    t_const = v([c4, c8], lambda: V.tensor_tensor(T.kk[:], T.k1[:], T.k2[:], A.max))
    t_vv = a([c7, t_vi], lambda: S.activation(T.vv[:], T.vi[:], IDENT, bias=T.t3f[:]))

    def quant_w(i):
        return v([t_w[i]], lambda: V.quantize_mx(T.wq[:, 512 * i:512 * i + 512], T.wp[:, 512 * i:512 * i + 512],
                                                 T.wm[:, 2048 * i:2048 * i + 2048]))
    for i in range(3):
        t_wq = quant_w(i)

    def score(s):
        return T.sc[:, 32 * s:32 * s + 32]

    def arrived(s):
        return [("s%d" % s, n_in[s])]
    conds = []
    for side, buf, cbuf, cmp in ((lambda s: s < r, T.mx1, T.cl1, A.is_gt), (lambda s: s > r, T.mx2, T.cl2, A.is_ge)):
        grp = [s for s in senders if side(s)]
        if not grp:
            continue
        cur, tk = score(grp[0]), []
        need("v", arrived(grp[0]))
        for n, s in enumerate(grp[1:]):
            nxt = buf[:] if n == 0 else T.win[:]
            tk = [v(tk + arrived(s), lambda: V.tensor_tensor(nxt, cur, score(s), A.max))]
            cur = nxt
        conds.append((cbuf, v(tk + [t_own], lambda: V.tensor_tensor(cbuf[:], score(r), cur, cmp))))
    if len(conds) == 2:
        wn_ = T.win
        t_win = v([conds[0][1], conds[1][1]], lambda: V.tensor_tensor(T.win[:], T.cl1[:], T.cl2[:], A.mult))
    else:
        wn_, t_win = conds[0]
    m16a, m32a = T.m16[:, 0:32], T.m32[:, 0:32]
    t1 = v([t_win, t_const], lambda: V.tensor_tensor_scan(T.ra[:], m32a, wn_[:], 0.0, A.mult, A.add))
    b1 = v([], lambda: V.tensor_tensor(T.w2[:], wn_[:], T.dl[:], A.mult))
    t2 = v([t1], lambda: V.transpose(T.rt[:, 32:64], T.ra[:]))
    b2 = v([b1], lambda: V.tensor_tensor(T.u2[:], T.dc[:], T.w2[:], A.subtract))
    t3 = v([t2], lambda: V.tensor_tensor_scan(T.ea[:], T.rt[:, 31:63], m16a, 0.0, A.add, A.mult))
    b3 = v([b2], lambda: V.tensor_tensor(T.ta[:], T.u2[:], T.ra[:], A.add))
    t4 = v([t3], lambda: V.transpose(T.et[:], T.ea[:]))
    m1 = v([], lambda: V.tensor_tensor(T.m64[:], T.sc[:, 0:64], T.sc[:, 64:128], A.max))
    t5 = v([t4, b3], lambda: V.tensor_scalar(T.oi[:], T.ta[:], T.et[:, 31:32], 1.25, A.add, A.mult))
    m2 = v([m1], lambda: V.tensor_tensor(T.mm[:], T.m64[:, 0:32], T.m64[:, 32:64], A.max))
    t6 = v([t5], lambda: V.tensor_copy(T.ou[:], T.oi[:]))
    n2 = v([m2], lambda: V.tensor_tensor(T.ne[:, 64:96], score(2), T.mm[:], A.not_equal))
    t7 = v([t6, t_vv], lambda: V.tensor_copy(T.ll[:].indirect(T.ou[:]), T.vv[:]))
    n1 = v([], lambda: V.tensor_tensor(T.ne[:, 32:64], score(1), T.mm[:], A.not_equal))
    t8 = v([t7], lambda: V.tensor_tensor_scan(T.sl5[:], T.ll[:, 0:240], T.kk[:], 4096.0, A.min, A.max))
    n0 = v([], lambda: V.tensor_tensor(T.ne[:, 0:32], score(0), T.mm[:], A.not_equal))
    t9 = v([t8], lambda: V.tensor_copy(T.offa[:], T.sl5[:, 3:240:5]))
    q2 = v([n2], lambda: V.tensor_scalar(T.q2[:], T.ne[:, 64:96], 1.0, None, A.add))
    t10 = a([t9], lambda: S.activation(T.cb[:, 384:768], T.xb[:].indirect(T.offa[:, 24:48]), COPY))
    t11 = v([t9], lambda: V.tensor_copy(T.cb[:, 0:384], T.xb[:].indirect(T.offa[:, 0:24])))
    q1 = v([q2, n1], lambda: V.tensor_tensor(T.q1[:], T.ne[:, 32:64], T.q2[:], A.mult))
    lo = CAP * r
    t_c = v([t10, t11], lambda: V.quantize_mx(T.lq[:, lo:lo + CAP], T.lp[:, lo:lo + CAP], T.cb[:]))
    need("g", [t_c])
    for d in peers:
        send(d, T.lq[:, lo:lo + CAP].bitcast(dt.uint8), "c%d" % r, "cloc")
        send(d, T.lp[:, lo:lo + CAP], "c%d" % r, "cloc")
    t_wq3 = quant_w(3)

    t = v([q1], lambda: V.tensor_scalar(T.q0[:], T.q1[:], 1.0, None, A.add))
    t_wn = v([t, n0], lambda: V.tensor_tensor(T.wnt[:], T.ne[:, 0:32], T.q0[:], A.mult))
    for s in range(NR):
        t = v([t_wn], lambda: V.tensor_scalar(T.ww[:, 32 * s:32 * s + 32], T.wnt[:], float(s), None, A.is_equal))
    t = v([t], lambda: V.tensor_tensor_scan(T.rr[:], T.m32[:], T.ww[:], 0.0, A.mult, A.add))
    t = v([t], lambda: V.transpose(T.rt4[:, 32:160], T.rr[:]))
    t = v([t], lambda: V.tensor_tensor_scan(T.e4[:], T.rt4[:, 31:159], T.m16[:], 0.0, A.add, A.mult))
    t = v([t], lambda: V.transpose(T.et4[:], T.e4[:]))
    for s in range(NR):
        c = 32 * s
        tp = v([t], lambda: V.tensor_scalar(T.p4[:, c:c + 32], T.rr[:, c:c + 32], T.et4[:, c + 31:c + 32],
                                            float(CAP * s - 1), A.add, A.add))
    t = v([tp], lambda: V.tensor_tensor(T.pm[:], T.p4[:], T.ww[:], A.mult))
    t = v([t], lambda: V.tensor_tensor(T.ph[:], T.pm[:, 0:64], T.pm[:, 64:128], A.add))
    t = v([t], lambda: V.tensor_tensor(T.pi[:], T.ph[:, 0:32], T.ph[:, 32:64], A.add))
    t_pt = v([t], lambda: V.transpose(T.ptr[:], T.pi[:]))
    for ab in range(4):
        for bh in range(2):
            p0, c0 = 32 * ab + 16 * bh, 128 * bh + 32 * ab
            t_d2 = dma("s", [t_pt], T.d2[0:16, c0:c0 + 32], T.ptr[p0:p0 + 16, :], "d2s")
    for k in range(8):
        t_zz = dma("s", [t_d2], T.zz[16 * k:16 * k + 16, :], T.d2[:], "zs")
    dma("s", [t_wn], T.wn[:], T.wnt[:], "wn")

    banks = {"v": [T.ps0, T.ps1, T.ps2, T.ps3], "a": [T.ps4, T.ps5, T.ps6, T.ps7]}
    hist = {"v": [], "a": []}
    ready = {}

    def product(s, h, o, e, deps):
        n = len(hist[e])
        bank = banks[e][n % 4]
        old = [hist[e][n - 4]] if n >= 4 else [t_own]
        w0, c0 = 256 * h + 128 * o, CAP * s
        tk = op("p", deps + old + [t_wq if h < 6 else t_wq3], lambda: g.tensor.matmul_mx(
            bank[:, 0:CAP], T.wq[:, w0:w0 + 128], T.wp[:, w0:w0 + 128], T.lq[:, c0:c0 + CAP], T.lp[:, c0:c0 + CAP],
            True, True), "p" + e)
        d0 = RW * (2 * h + o) + c0
        if e == "v":
            c = v([tk], lambda: V.tensor_copy(T.rw[:, d0:d0 + CAP], bank[:, 0:CAP]))
        else:
            c = a([tk], lambda: S.activation(T.rw[:, d0:d0 + CAP], bank[:, 0:CAP], COPY))
        hist[e].append(c)
        ready[(s, h, o)] = c

    def window(h, o):
        d0 = RW * (2 * h + o)
        return T.rw[:, d0:d0 + RW]

    def rdeps(h, o):
        return [ready[(s, h, o)] for s in range(NR)]

    jobs = [(h, o) for h in range(8) for o in range(2)]
    for n, (h, o) in enumerate(jobs):
        product(r, h, o, "v" if n % 4 == 3 else "a", [t_c])
    for s in senders[:2]:
        for n, (h, o) in enumerate(jobs):
            product(s, h, o, "v" if n % 2 else "a", [("c%d" % s, 2 * n_in[s])])
    for bh in range(2):
        t_ob = v([t_zz], lambda: V.tensor_copy(T.offb[:, bh:256:2], T.zz[:, 128 * bh:128 * bh + 128]))
    s = senders[2]
    dep = [("c%d" % s, 2 * n_in[s])]

    def gath(out, h, o):
        return a(rdeps(h, o) + [t_ob], lambda: S.activation(out[:], window(h, o).indirect(T.offb[:, 32 * h:32 * h + 32]), COPY))
    for h, o, e in ((7, 0, "a"), (0, 0, "v"), (1, 0, "v")):
        product(s, h, o, e, dep)
    t_g0 = gath(T.g0, 7, 0)
    for h, o, e in ((5, 0, "a"), (2, 0, "v"), (3, 0, "v"), (6, 0, "a"), (4, 0, "v"), (0, 1, "v"), (1, 1, "v")):
        product(s, h, o, e, dep)
    t_g5 = gath(T.g5, 5, 0)
    t_g6 = gath(T.g6, 6, 0)
    t_ga = op("g", [t_g5, t_g6], lambda: g.dma_start(T.g6[:], T.g5[:], accum_op=A.add), "ga", 16)
    product(s, 7, 1, "a", dep)
    t_g1 = gath(T.g1, 7, 1)
    for h in (2, 3, 4, 5, 6):
        product(s, h, 1, "a", dep)

    cur, tk = T.g0, [t_g0]
    for h in range(5):
        out = (T.ac0, T.ac1)[h % 2]
        tk = [v(tk + rdeps(h, 0) + [t_ob], lambda: V.tensor_tensor(
            out[:], window(h, 0).indirect(T.offb[:, 32 * h:32 * h + 32]), cur[:], A.add))]
        cur = out
    t_y0 = dma("s", tk, T.y[:, 0:512], cur[:], "y0")
    op("g", [t_ga, t_y0], lambda: g.dma_start(T.y[:, 0:512], T.g6[:], accum_op=A.add), "ga", 16)
    cur, tk = T.g1, [t_g1]
    for h in range(6):
        out = (T.ac2, T.ac3)[h % 2]
        tk = [v(tk + rdeps(h, 1), lambda: V.tensor_tensor(
            out[:], window(h, 1).indirect(T.offb[:, 32 * h:32 * h + 32]), cur[:], A.add))]
        cur = out
    for k in range(2):
        c0 = 256 * k
        t_l = v(tk + rdeps(6, 1), lambda: V.tensor_tensor(
            T.ac2[:, c0:c0 + 256], window(6, 1).indirect(T.offb[:, 192 + 16 * k:192 + 16 * k + 16]), cur[:, c0:c0 + 256], A.add))
        dma(("s", "a")[k], [t_l], T.y[:, 512 + c0:768 + c0], T.ac2[:, c0:c0 + 256], "y%d" % (1 + k))

    need("g", sorted(cnt.items()))
